import numpy as np
import ml_dtypes


def mxq(x, axis, fmt="e4m3"):
    dtype, down = {"e4m3": (ml_dtypes.float8_e4m3fn, 7), "e5m2": (ml_dtypes.float8_e5m2, 14)}[fmt]
    v = np.moveaxis(np.asarray(x, np.float32).astype(ml_dtypes.bfloat16).astype(np.float64), axis, -1)
    blocks = v.reshape(v.shape[:-1] + (-1, 32))
    amax = np.abs(blocks).max(-1, keepdims=True)
    byte = np.maximum(np.where(amax > 0, np.frexp(amax)[1] - 1 + 127, 0) - down, 1)
    scale = np.exp2(byte - 127.0)
    codes = (blocks / scale).astype(np.float32).astype(dtype).astype(np.float64)
    return np.moveaxis((codes * scale).reshape(v.shape), -1, axis)


WIDE = False


def mx_kscale(k):
    if not WIDE:
        return np.ones(k)
    levels = np.array([10, -10, 5, -5, 0])
    if k % 512:
        return np.exp2(np.random.permutation(np.resize(levels, k // 32))).repeat(32)
    a = np.empty((k // 512, 16))
    for p in range(k // 512):
        a[p, :8] = np.random.permutation(np.resize(levels, 8))
        for g in range(8):
            far = levels[np.abs(levels - a[p, g]) >= 10]
            a[p, g + 8] = far[np.random.randint(len(far))]
    return np.exp2(a.ravel()).repeat(32)


def f64(x):
    return np.asarray(x).astype(np.float64)


def striped(idx):
    return np.tile(np.asarray(idx).reshape(-1, 16).T, (8, 1)).astype(np.uint16)


def unstriped(offs):
    return offs[:16].T.reshape(-1).astype(np.int64)


E2M1 = np.array([0.0, 0.5, 1.0, 1.5, 2.0, 3.0, 4.0, 6.0, -0.0, -0.5, -1.0, -1.5, -2.0, -3.0, -4.0, -6.0])


def pack_weight(w, fmt):
    k, n = w.shape
    w = f64(np.asarray(w, np.float32).astype(ml_dtypes.bfloat16)).reshape(k // 32, 32, n)
    amax = np.abs(w).max(1)
    if fmt == "e4m3":
        byte = np.frexp(amax)[1] - 1 + 127 - 7
    else:
        mant, ex = np.frexp(amax / 6.0)
        byte = np.where(mant > 0.5, ex, ex - 1) + 127
    byte = np.clip(np.where(amax > 0, byte, 1), 1, 254)
    scaled = (w * np.exp2(127.0 - byte)[:, None, :]).reshape(k, n).astype(np.float32)
    by_word = np.ascontiguousarray(scaled.reshape(k // 512, 128, 4, n).transpose(0, 1, 3, 2))
    if fmt == "e4m3":
        words = by_word.astype(ml_dtypes.float8_e4m3fn).view(np.uint8)
    else:
        c = by_word.astype(ml_dtypes.float4_e2m1fn).view(np.uint8) & 0xF
        words = (c[..., 0::2] | (c[..., 1::2] << 4)).reshape(k // 512, 128, 2 * n)
    return np.ascontiguousarray(words), np.ascontiguousarray(byte.astype(np.uint8).reshape(k // 512, 16, n))


def unpack_weight(words, scales, fmt):
    g, _, n = scales.shape
    words = np.ascontiguousarray(words).reshape(g, 128, n, -1)
    if fmt == "e4m3":
        vals = words.view(ml_dtypes.float8_e4m3fn).astype(np.float64)
    else:
        nib = np.empty((g, 128, n, 4), np.uint8)
        nib[..., 0::2] = words & 0xF
        nib[..., 1::2] = words >> 4
        vals = E2M1[nib]
    vals = vals * np.repeat(np.exp2(scales.astype(np.float64) - 127.0), 8, axis=1)[..., None]
    return vals.transpose(0, 1, 3, 2).reshape(g * 512, n)


def bf(x):
    return np.asarray(x, np.float32).astype(ml_dtypes.bfloat16)


def planes(Y):
    r, m = Y.shape
    b = f64(bf(Y)).reshape(r // 32, 32, m)
    amax = np.abs(b).max(1)
    byte = np.clip(np.where(amax > 0, np.frexp(amax)[1] - 1 + 127 - 7, 1), 1, 254)
    codes = (b * np.exp2(127.0 - byte)[:, None, :]).reshape(r, m).astype(np.float32).astype(ml_dtypes.float8_e4m3fn).view(np.uint8)
    words = codes.reshape(r // 512, 128, 4, m).transpose(0, 1, 3, 2)
    return np.ascontiguousarray(words), np.ascontiguousarray(byte.astype(np.uint8).reshape(r // 512, 16, m))


K, T, J, N = 512, 512, 512, 512


def setup_inputs():
    n = np.random.standard_normal
    idx = np.random.randint(0, T, J)
    idx2 = np.random.randint(0, T, J)
    fk = mx_kscale(K)
    wap = pack_weight(n((K, N)) * 1 / np.sqrt(K) * fk[:, None], "e2m1")
    wbp = pack_weight(n((K, N)) * 1 / np.sqrt(K) * fk[:, None], "e4m3")
    return {
        "xt": (n((K, T)) / fk[:, None]).astype(np.float32),
        "wa_words": wap[0],
        "wa_scales": wap[1],
        "wb_words": wbp[0],
        "wb_scales": wbp[1],
        "sh": (np.random.uniform(0.1, 0.4, (N, 1))).astype(np.float32),
        "offs": striped(idx),
        "offs2": striped(idx2),
    }


def reference(xt, wa_words, wa_scales, wb_words, wb_scales, sh, offs, offs2):
    idx = unstriped(offs)
    idx2 = unstriped(offs2)
    wau = unpack_weight(wa_words, wa_scales, "e2m1")
    wbu = unpack_weight(wb_words, wb_scales, "e4m3")
    xtq = mxq(f64(xt), 0, "e4m3")
    z = wau.T @ xtq
    u = wbu.T @ xtq
    y = z[:, idx] / (1.0 + np.maximum(u[:, idx2], 0.0)) + f64(sh) * u[:, idx]
    words, scales = planes(y)
    return y, words, scales

@@ -1,0 +1,150 @@
+from contextlib import ExitStack
+
+import concourse.mybir as mybir
+
+K, T, J, N = 512, 512, 512, 512
+FLOPS = 2 * 2 * K * N * T
+
+F32 = mybir.dt.float32
+BF16 = mybir.dt.bfloat16
+I32 = mybir.dt.int32
+U16 = mybir.dt.uint16
+U8 = mybir.dt.uint8
+FP8X4 = mybir.dt.float8_e4m3fn_x4
+FP4X4 = mybir.dt.float4_e2m1fn_x4
+ACT = mybir.ActivationFunctionType
+ALU = mybir.AluOpType
+
+P = 128
+PACK = 4
+HALF = T // 2
+U_WINDOW = 704
+CHUNKS = ((0, 256), (256, 512))
+X_VECTOR_COLS = 160
+ROOT = 1.0625
+
+
+def tile_list_divided_by_neighbour_pl_kernel(tc, xt, wa_words, wa_scales, wb_words, wb_scales, sh, offs, offs2, out_0, out_1, out_2):
+    nc = tc.nc
+    with ExitStack() as ctx:
+        keep = ctx.enter_context(tc.tile_pool(name="keep", bufs=1))
+        psum = ctx.enter_context(tc.psum_pool(name="psum", bufs=1))
+
+        def tile(shape, dtype, name):
+            return keep.tile(shape, dtype, name=name, align_bytes=64)
+
+        offs_sb = keep.tile([P, J // 16], U16, name="offs_sb")
+        offs2_sb = keep.tile([P, J // 16], U16, name="offs2_sb")
+
+        warm_in = tile([P, 1], F32, "warm_in")
+        warm_out = tile([P, 1], F32, "warm_out")
+        nc.vector.memset(warm_in[:], 1.0)
+        nc.scalar.activation(out=warm_out[:], in_=warm_in[:], func=ACT.Abs_reciprocal_sqrt)
+
+        sb_raw = tile([P, N], U8, "sb_raw")
+        sa_raw = tile([P, N], U8, "sa_raw")
+        nc.gpsimd.memset(sb_raw[:].bitcast(I32), 0)
+        nc.gpsimd.memset(sa_raw[:].bitcast(I32), 0)
+        centre = tile([P, 1], F32, "centre")
+        nc.vector.memset(centre[:], ROOT * ROOT)
+
+        x_rows = xt.rearrange("(p i) w -> p i w", i=PACK)
+        x_raw = [tile([P, PACK, HALF], F32, "x_raw%d" % h) for h in range(2)]
+        wb_raw = tile([P, N], I32, "wb_raw")
+        wa_raw = tile([P, 2 * N], U8, "wa_raw")
+        sh_sb = tile([P, PACK], F32, "sh_sb")
+
+        nc.sync.dma_start(out=x_raw[0][:], in_=x_rows[:, :, 0:HALF])
+        nc.sync.dma_start(out=wb_raw[:], in_=wb_words[0].rearrange("p n r -> p (n r)").bitcast(I32))
+        for q in range(4):
+            nc.scalar.dma_start(out=sb_raw[:].bitcast(I32)[32 * q : 32 * q + 4, :], in_=wb_scales[0].bitcast(I32)[4 * q : 4 * q + 4, :])
+        nc.sync.dma_start(out=x_raw[1][:], in_=x_rows[:, :, HALF:T])
+        nc.sync.dma_start(out=wa_raw[:].bitcast(I32), in_=wa_words[0].bitcast(I32))
+        nc.sync.dma_start(offs2_sb[:], offs2)
+        for q in range(4):
+            nc.sync.dma_start(out=sa_raw[:].bitcast(I32)[32 * q : 32 * q + 4, :], in_=wa_scales[0].bitcast(I32)[4 * q : 4 * q + 4, :])
+        nc.sync.dma_start(offs_sb[:], offs)
+        nc.sync.dma_start(out=sh_sb[:], in_=sh.rearrange("(p t) o -> p (t o)", t=PACK))
+
+        u_sb = [tile([P, U_WINDOW], F32, "u_sb%d" % t) for t in range(PACK)]
+        z_sb = [tile([P, T], F32, "z_sb%d" % t) for t in range(PACK)]
+        for t in range(PACK):
+            nc.gpsimd.memset(u_sb[t][:, T:U_WINDOW], 0.0)
+
+        wb_dealt = tile([P, N], I32, "wb_dealt")
+        sb_dealt = tile([P, N], U8, "sb_dealt")
+        wa_dealt = tile([P, 2 * N], U8, "wa_dealt")
+        sa_dealt = tile([P, N], U8, "sa_dealt")
+
+        def deal(dst, src):
+            nc.vector.tensor_copy(out=dst.rearrange("p (t m) -> p t m", t=PACK), in_=src.rearrange("p (m t) -> p t m", t=PACK))
+
+        deal(wb_dealt[:], wb_raw[:])
+        deal(sb_dealt[:], sb_raw[:])
+
+        x_bf = [tile([P, HALF, PACK], BF16, "x_bf%d" % h) for h in range(2)]
+        x_codes = tile([P, T], I32, "x_codes")
+        x_scales = tile([P, T], U8, "x_scales")
+
+        def weave(copy, dst, src, lo, hi):
+            copy(out=dst[:, lo:hi, :].rearrange("p (c i) t -> p c t i", i=4), in_=src[:, :, lo:hi].rearrange("p t (c i) -> p c t i", i=4))
+
+        u_ps = [psum.tile([P, T], F32, name="u_ps%d" % t) for t in range(PACK)]
+        z_ps = [psum.tile([P, T], F32, name="z_ps%d" % t) for t in range(PACK)]
+
+        for h in range(2):
+            cols = slice(h * HALF, (h + 1) * HALF)
+            weave(nc.scalar.copy, x_bf[h], x_raw[h], X_VECTOR_COLS, HALF)
+            weave(nc.vector.tensor_copy, x_bf[h], x_raw[h], 0, X_VECTOR_COLS)
+            nc.vector.quantize_mx(out=x_codes[:, cols].bitcast(FP8X4), scales=x_scales[:, cols], in_=x_bf[h][:].rearrange("p c t -> p (c t)"))
+            for t in range(PACK):
+                m = slice(t * P, (t + 1) * P)
+                nc.tensor.matmul_mx(out=u_ps[t][:, cols], lhsT=wb_dealt[:, m].bitcast(FP8X4), lhsT_scale=sb_dealt[:, m],
+                                    rhs=x_codes[:, cols].bitcast(FP8X4), rhs_scale=x_scales[:, cols], start=True, stop=True)
+            if h == 0:
+                deal(wa_dealt[:].bitcast(U16), wa_raw[:].bitcast(U16))
+        deal(sa_dealt[:], sa_raw[:])
+        for t in range(PACK):
+            nc.scalar.copy(out=u_sb[t][:, 0:T], in_=u_ps[t][:])
+        for t in range(PACK):
+            nc.tensor.matmul_mx(out=z_ps[t][:], lhsT=wa_dealt[:, 2 * t * P : 2 * (t + 1) * P].bitcast(FP4X4), lhsT_scale=sa_dealt[:, t * P : (t + 1) * P],
+                                rhs=x_codes[:].bitcast(FP8X4), rhs_scale=x_scales[:], start=True, stop=True)
+
+        drive = [tile([P, J], F32, "drive%d" % t) for t in range(PACK)]
+        own = [tile([P, J], F32, "own%d" % t) for t in range(PACK)]
+        pos = [tile([P, J], F32, "pos%d" % t) for t in range(PACK)]
+        root = [tile([P, J], F32, "root%d" % t) for t in range(PACK)]
+        gain = [tile([P, J], F32, "gain%d" % t) for t in range(PACK)]
+        for t in range(PACK):
+            nc.vector.tensor_copy(out=drive[t][:], in_=u_sb[t][:].indirect(offs2_sb[:]))
+        for t in range(PACK):
+            nc.scalar.copy(out=z_sb[t][:], in_=z_ps[t][:])
+        for t in range(PACK):
+            nc.vector.tensor_copy(out=own[t][:], in_=u_sb[t][:].indirect(offs_sb[:]))
+        for t in range(PACK):
+            nc.scalar.activation(out=pos[t][:], in_=drive[t][:], func=ACT.Relu)
+            nc.scalar.activation(out=root[t][:], in_=pos[t][:], func=ACT.Abs_reciprocal_sqrt, scale=ROOT * ROOT, bias=centre[:])
+            nc.scalar.activation(out=gain[t][:], in_=root[t][:], func=ACT.Square, scale=ROOT)
+
+        y_rows = out_0.rearrange("(p t) j -> p t j", t=PACK)
+        y_codes = tile([P, J], I32, "y_codes")
+        y_scales = tile([P, J], U8, "y_scales")
+        words_out = out_1[0].rearrange("p c r -> p (c r)").bitcast(I32)
+        for c, (lo, hi) in enumerate(CHUNKS):
+            w = hi - lo
+            y = tile([P, PACK, w], F32, "y%d" % c)
+            y_bf = tile([P, w, PACK], BF16, "y_bf%d" % c)
+            quot = [tile([P, w], F32, "quot%d_%d" % (c, t)) for t in range(PACK)]
+            for t in range(PACK + 1):
+                if t < PACK:
+                    nc.vector.tensor_tensor(out=quot[t][:], in0=z_sb[t][:].indirect(offs_sb[:, lo // 16 : hi // 16]), in1=gain[t][:, lo:hi], op=ALU.mult)
+                if t > 0:
+                    s = t - 1
+                    nc.vector.scalar_tensor_tensor(out=y[:, s, :], in0=own[s][:, lo:hi], scalar=sh_sb[:, s : s + 1], in1=quot[s][:], op0=ALU.mult, op1=ALU.add)
+                    nc.sync.dma_start(out=y_rows[:, s, lo:hi], in_=y[:, s, :])
+            weave(nc.scalar.copy if c < len(CHUNKS) - 1 else nc.vector.tensor_copy, y_bf, y, 0, w)
+            nc.vector.quantize_mx(out=y_codes[:, lo:hi].bitcast(FP8X4), scales=y_scales[:, lo:hi], in_=y_bf[:].rearrange("p c t -> p (c t)"))
+            nc.sync.dma_start(out=words_out[:, lo:hi], in_=y_codes[:, lo:hi])
+        for q in range(4):
+            queue = nc.scalar if q % 2 == 0 else nc.sync
+            queue.dma_start(out=out_2[0].bitcast(I32)[4 * q : 4 * q + 4, :], in_=y_scales[:].bitcast(I32)[32 * q : 32 * q + 4, :])

@@ -19,7 +19,7 @@ P = 128
 PACK = 4
 HALF = T // 2
 U_WINDOW = 704
-CHUNKS = ((0, 256), (256, 512))
+CHUNKS = ((0, 256), (256, 384), (384, 512))
 X_VECTOR_COLS = 160
 ROOT = 1.0625
 
@@ -30,21 +30,14 @@ def tile_list_divided_by_neighbour_pl_kernel(tc, xt, wa_words, wa_scales, wb_wor
         keep = ctx.enter_context(tc.tile_pool(name="keep", bufs=1))
         psum = ctx.enter_context(tc.psum_pool(name="psum", bufs=1))
 
-        def tile(shape, dtype, name):
-            return keep.tile(shape, dtype, name=name, align_bytes=64)
+        def tile(shape, dtype, name, tag=None):
+            return keep.tile(shape, dtype, name=name, tag=tag or name, align_bytes=64)
 
         offs_sb = keep.tile([P, J // 16], U16, name="offs_sb")
         offs2_sb = keep.tile([P, J // 16], U16, name="offs2_sb")
 
-        warm_in = tile([P, 1], F32, "warm_in")
-        warm_out = tile([P, 1], F32, "warm_out")
-        nc.vector.memset(warm_in[:], 1.0)
-        nc.scalar.activation(out=warm_out[:], in_=warm_in[:], func=ACT.Abs_reciprocal_sqrt)
-
         sb_raw = tile([P, N], U8, "sb_raw")
         sa_raw = tile([P, N], U8, "sa_raw")
-        nc.gpsimd.memset(sb_raw[:].bitcast(I32), 0)
-        nc.gpsimd.memset(sa_raw[:].bitcast(I32), 0)
         centre = tile([P, 1], F32, "centre")
         nc.vector.memset(centre[:], ROOT * ROOT)
 
@@ -54,17 +47,27 @@ def tile_list_divided_by_neighbour_pl_kernel(tc, xt, wa_words, wa_scales, wb_wor
         wa_raw = tile([P, 2 * N], U8, "wa_raw")
         sh_sb = tile([P, PACK], F32, "sh_sb")
 
+        def load_scales(queue, plane, rows, q):
+            queue.dma_start(out=plane[:].bitcast(I32)[32 * q : 32 * q + 4, :], in_=rows[0].bitcast(I32)[4 * q : 4 * q + 4, :])
+
+        nc.gpsimd.memset(sb_raw[:].bitcast(I32), 0)
+        nc.gpsimd.memset(sa_raw[:].bitcast(I32), 0)
         nc.sync.dma_start(out=x_raw[0][:], in_=x_rows[:, :, 0:HALF])
         nc.sync.dma_start(out=wb_raw[:], in_=wb_words[0].rearrange("p n r -> p (n r)").bitcast(I32))
         for q in range(4):
-            nc.scalar.dma_start(out=sb_raw[:].bitcast(I32)[32 * q : 32 * q + 4, :], in_=wb_scales[0].bitcast(I32)[4 * q : 4 * q + 4, :])
+            load_scales(nc.scalar, sb_raw, wb_scales, q)
         nc.sync.dma_start(out=x_raw[1][:], in_=x_rows[:, :, HALF:T])
-        nc.sync.dma_start(out=wa_raw[:].bitcast(I32), in_=wa_words[0].bitcast(I32))
         nc.sync.dma_start(offs2_sb[:], offs2)
+        nc.sync.dma_start(out=wa_raw[:].bitcast(I32), in_=wa_words[0].bitcast(I32))
         for q in range(4):
-            nc.sync.dma_start(out=sa_raw[:].bitcast(I32)[32 * q : 32 * q + 4, :], in_=wa_scales[0].bitcast(I32)[4 * q : 4 * q + 4, :])
+            load_scales(nc.sync, sa_raw, wa_scales, q)
         nc.sync.dma_start(offs_sb[:], offs)
-        nc.sync.dma_start(out=sh_sb[:], in_=sh.rearrange("(p t) o -> p (t o)", t=PACK))
+        nc.gpsimd.dma_start(out=sh_sb[:], in_=sh.rearrange("(p t) o -> p (t o)", t=PACK))
+
+        warm_in = tile([P, 1], F32, "warm_in")
+        warm_out = tile([P, 1], F32, "warm_out")
+        nc.gpsimd.memset(warm_in[:], 1.0)
+        nc.scalar.activation(out=warm_out[:], in_=warm_in[:], func=ACT.Abs_reciprocal_sqrt)
 
         u_sb = [tile([P, U_WINDOW], F32, "u_sb%d" % t) for t in range(PACK)]
         z_sb = [tile([P, T], F32, "z_sb%d" % t) for t in range(PACK)]
@@ -76,8 +79,8 @@ def tile_list_divided_by_neighbour_pl_kernel(tc, xt, wa_words, wa_scales, wb_wor
         wa_dealt = tile([P, 2 * N], U8, "wa_dealt")
         sa_dealt = tile([P, N], U8, "sa_dealt")
 
-        def deal(dst, src):
-            nc.vector.tensor_copy(out=dst.rearrange("p (t m) -> p t m", t=PACK), in_=src.rearrange("p (m t) -> p t m", t=PACK))
+        def deal(dst, src, engine=nc.vector):
+            engine.tensor_copy(out=dst.rearrange("p (t m) -> p t m", t=PACK), in_=src.rearrange("p (m t) -> p t m", t=PACK))
 
         deal(wb_dealt[:], wb_raw[:])
         deal(sb_dealt[:], sb_raw[:])
@@ -89,28 +92,25 @@ def tile_list_divided_by_neighbour_pl_kernel(tc, xt, wa_words, wa_scales, wb_wor
         def weave(copy, dst, src, lo, hi):
             copy(out=dst[:, lo:hi, :].rearrange("p (c i) t -> p c t i", i=4), in_=src[:, :, lo:hi].rearrange("p t (c i) -> p c t i", i=4))
 
-        u_ps = [psum.tile([P, T], F32, name="u_ps%d" % t) for t in range(PACK)]
-        z_ps = [psum.tile([P, T], F32, name="z_ps%d" % t) for t in range(PACK)]
 
         for h in range(2):
             cols = slice(h * HALF, (h + 1) * HALF)
-            weave(nc.scalar.copy, x_bf[h], x_raw[h], X_VECTOR_COLS, HALF)
-            weave(nc.vector.tensor_copy, x_bf[h], x_raw[h], 0, X_VECTOR_COLS)
+            weave(nc.vector.tensor_copy, x_bf[h], x_raw[h], 0, HALF)
             nc.vector.quantize_mx(out=x_codes[:, cols].bitcast(FP8X4), scales=x_scales[:, cols], in_=x_bf[h][:].rearrange("p c t -> p (c t)"))
             for t in range(PACK):
                 m = slice(t * P, (t + 1) * P)
-                nc.tensor.matmul_mx(out=u_ps[t][:, cols], lhsT=wb_dealt[:, m].bitcast(FP8X4), lhsT_scale=sb_dealt[:, m],
+                u_ps = psum.tile([P, T], F32, name="u_ps%d_%d" % (h, t), tag="bank%d" % (PACK * h + t))
+                nc.tensor.matmul_mx(out=u_ps[:, 0:HALF], lhsT=wb_dealt[:, m].bitcast(FP8X4), lhsT_scale=sb_dealt[:, m],
                                     rhs=x_codes[:, cols].bitcast(FP8X4), rhs_scale=x_scales[:, cols], start=True, stop=True)
-            if h == 0:
-                deal(wa_dealt[:].bitcast(U16), wa_raw[:].bitcast(U16))
-        deal(sa_dealt[:], sa_raw[:])
-        for t in range(PACK):
-            nc.scalar.copy(out=u_sb[t][:, 0:T], in_=u_ps[t][:])
+                nc.scalar.copy(out=u_sb[t][:, cols], in_=u_ps[:, 0:HALF])
+        deal(wa_dealt[:].bitcast(U16), wa_raw[:].bitcast(U16))
+        deal(sa_dealt[:], sa_raw[:], nc.gpsimd)
+        z_ps = [psum.tile([P, T], F32, name="z_ps%d" % t, tag="bank%d" % t) for t in range(PACK)]
         for t in range(PACK):
             nc.tensor.matmul_mx(out=z_ps[t][:], lhsT=wa_dealt[:, 2 * t * P : 2 * (t + 1) * P].bitcast(FP4X4), lhsT_scale=sa_dealt[:, t * P : (t + 1) * P],
                                 rhs=x_codes[:].bitcast(FP8X4), rhs_scale=x_scales[:], start=True, stop=True)
 
-        drive = [tile([P, J], F32, "drive%d" % t) for t in range(PACK)]
+        drive = [tile([P, J], F32, "drive%d" % t, tag="wa_raw" if t == 0 else None) for t in range(PACK)]
         own = [tile([P, J], F32, "own%d" % t) for t in range(PACK)]
         pos = [tile([P, J], F32, "pos%d" % t) for t in range(PACK)]
         root = [tile([P, J], F32, "root%d" % t) for t in range(PACK)]
@@ -121,27 +121,34 @@ def tile_list_divided_by_neighbour_pl_kernel(tc, xt, wa_words, wa_scales, wb_wor
             nc.scalar.copy(out=z_sb[t][:], in_=z_ps[t][:])
         for t in range(PACK):
             nc.vector.tensor_copy(out=own[t][:], in_=u_sb[t][:].indirect(offs_sb[:]))
-        for t in range(PACK):
-            nc.scalar.activation(out=pos[t][:], in_=drive[t][:], func=ACT.Relu)
-            nc.scalar.activation(out=root[t][:], in_=pos[t][:], func=ACT.Abs_reciprocal_sqrt, scale=ROOT * ROOT, bias=centre[:])
-            nc.scalar.activation(out=gain[t][:], in_=root[t][:], func=ACT.Square, scale=ROOT)
+        for step in range(PACK + 2):
+            if step < PACK:
+                nc.scalar.activation(out=pos[step][:], in_=drive[step][:], func=ACT.Relu)
+            if 1 <= step <= PACK:
+                nc.scalar.activation(out=root[step - 1][:], in_=pos[step - 1][:], func=ACT.Abs_reciprocal_sqrt, scale=ROOT * ROOT, bias=centre[:])
+            if step >= 2:
+                nc.scalar.activation(out=gain[step - 2][:], in_=root[step - 2][:], func=ACT.Square, scale=ROOT)
 
         y_rows = out_0.rearrange("(p t) j -> p t j", t=PACK)
         y_codes = tile([P, J], I32, "y_codes")
         y_scales = tile([P, J], U8, "y_scales")
         words_out = out_1[0].rearrange("p c r -> p (c r)").bitcast(I32)
+        ring = [tile([P, HALF], F32, "quot%d" % r) for r in range(3)]
         for c, (lo, hi) in enumerate(CHUNKS):
             w = hi - lo
             y = tile([P, PACK, w], F32, "y%d" % c)
             y_bf = tile([P, w, PACK], BF16, "y_bf%d" % c)
-            quot = [tile([P, w], F32, "quot%d_%d" % (c, t)) for t in range(PACK)]
+            quot = [ring[(PACK * c + t) % 3][:, 0:w] for t in range(PACK)]
+            if c == 2:
+                quot[0] = tile([P, w], F32, "quot_a", tag="y_bf0")[:]
+                quot[3] = tile([P, w], F32, "quot_b", tag="y_bf1")[:]
             for t in range(PACK + 1):
                 if t < PACK:
-                    nc.vector.tensor_tensor(out=quot[t][:], in0=z_sb[t][:].indirect(offs_sb[:, lo // 16 : hi // 16]), in1=gain[t][:, lo:hi], op=ALU.mult)
+                    nc.vector.tensor_tensor(out=quot[t], in0=z_sb[t][:].indirect(offs_sb[:, lo // 16 : hi // 16]), in1=gain[t][:, lo:hi], op=ALU.mult)
                 if t > 0:
                     s = t - 1
-                    nc.vector.scalar_tensor_tensor(out=y[:, s, :], in0=own[s][:, lo:hi], scalar=sh_sb[:, s : s + 1], in1=quot[s][:], op0=ALU.mult, op1=ALU.add)
-                    nc.sync.dma_start(out=y_rows[:, s, lo:hi], in_=y[:, s, :])
+                    nc.vector.scalar_tensor_tensor(out=y[:, s, :], in0=own[s][:, lo:hi], scalar=sh_sb[:, s : s + 1], in1=quot[s], op0=ALU.mult, op1=ALU.add)
+            nc.sync.dma_start(out=y_rows[:, :, lo:hi], in_=y[:])
             weave(nc.scalar.copy if c < len(CHUNKS) - 1 else nc.vector.tensor_copy, y_bf, y, 0, w)
             nc.vector.quantize_mx(out=y_codes[:, lo:hi].bitcast(FP8X4), scales=y_scales[:, lo:hi], in_=y_bf[:].rearrange("p c t -> p (c t)"))
             nc.sync.dma_start(out=words_out[:, lo:hi], in_=y_codes[:, lo:hi])

@@ -20,7 +20,8 @@ PACK = 4
 HALF = T // 2
 U_WINDOW = 704
 CHUNKS = ((0, 256), (256, 384), (384, 512))
-X_VECTOR_COLS = 160
+X_CHUNKS = ((0, 256), (256, 384), (384, 512))
+X_SPLIT = 160
 ROOT = 1.0625
 
 
@@ -42,25 +43,25 @@ def tile_list_divided_by_neighbour_pl_kernel(tc, xt, wa_words, wa_scales, wb_wor
         nc.vector.memset(centre[:], ROOT * ROOT)
 
         x_rows = xt.rearrange("(p i) w -> p i w", i=PACK)
-        x_raw = [tile([P, PACK, HALF], F32, "x_raw%d" % h) for h in range(2)]
+        x_raw = [tile([P, PACK, hi - lo], F32, "x_raw%d" % h) for h, (lo, hi) in enumerate(X_CHUNKS)]
         wb_raw = tile([P, N], I32, "wb_raw")
         wa_raw = tile([P, 2 * N], U8, "wa_raw")
         sh_sb = tile([P, PACK], F32, "sh_sb")
 
-        def load_scales(queue, plane, rows, q):
-            queue.dma_start(out=plane[:].bitcast(I32)[32 * q : 32 * q + 4, :], in_=rows[0].bitcast(I32)[4 * q : 4 * q + 4, :])
+        def load_scales(queue, plane, rows):
+            for q in range(4):
+                queue.dma_start(out=plane[:].bitcast(I32)[32 * q : 32 * q + 4, :], in_=rows[0].bitcast(I32)[4 * q : 4 * q + 4, :])
 
         nc.gpsimd.memset(sb_raw[:].bitcast(I32), 0)
         nc.gpsimd.memset(sa_raw[:].bitcast(I32), 0)
-        nc.sync.dma_start(out=x_raw[0][:], in_=x_rows[:, :, 0:HALF])
         nc.sync.dma_start(out=wb_raw[:], in_=wb_words[0].rearrange("p n r -> p (n r)").bitcast(I32))
-        for q in range(4):
-            load_scales(nc.scalar, sb_raw, wb_scales, q)
-        nc.sync.dma_start(out=x_raw[1][:], in_=x_rows[:, :, HALF:T])
+        nc.sync.dma_start(out=x_raw[0][:], in_=x_rows[:, :, X_CHUNKS[0][0] : X_CHUNKS[0][1]])
+        load_scales(nc.sync, sb_raw, wb_scales)
+        for h in range(1, len(X_CHUNKS)):
+            nc.sync.dma_start(out=x_raw[h][:], in_=x_rows[:, :, X_CHUNKS[h][0] : X_CHUNKS[h][1]])
         nc.sync.dma_start(offs2_sb[:], offs2)
         nc.sync.dma_start(out=wa_raw[:].bitcast(I32), in_=wa_words[0].bitcast(I32))
-        for q in range(4):
-            load_scales(nc.sync, sa_raw, wa_scales, q)
+        load_scales(nc.sync, sa_raw, wa_scales)
         nc.sync.dma_start(offs_sb[:], offs)
         nc.gpsimd.dma_start(out=sh_sb[:], in_=sh.rearrange("(p t) o -> p (t o)", t=PACK))
 
@@ -79,33 +80,43 @@ def tile_list_divided_by_neighbour_pl_kernel(tc, xt, wa_words, wa_scales, wb_wor
         wa_dealt = tile([P, 2 * N], U8, "wa_dealt")
         sa_dealt = tile([P, N], U8, "sa_dealt")
 
-        def deal(dst, src, engine=nc.vector):
-            engine.tensor_copy(out=dst.rearrange("p (t m) -> p t m", t=PACK), in_=src.rearrange("p (m t) -> p t m", t=PACK))
+        def deal(dst, src, line, engine=nc.vector):
+            engine.tensor_copy(out=dst.rearrange("p (t a i) -> p a t i", t=PACK, i=line), in_=src.rearrange("p (a i t) -> p a t i", t=PACK, i=line))
 
-        deal(wb_dealt[:], wb_raw[:])
-        deal(sb_dealt[:], sb_raw[:])
+        deal(wb_dealt[:], wb_raw[:], 4)
+        deal(sb_dealt[:], sb_raw[:], 16)
 
         x_bf = [tile([P, HALF, PACK], BF16, "x_bf%d" % h) for h in range(2)]
         x_codes = tile([P, T], I32, "x_codes")
         x_scales = tile([P, T], U8, "x_scales")
 
-        def weave(copy, dst, src, lo, hi):
-            copy(out=dst[:, lo:hi, :].rearrange("p (c i) t -> p c t i", i=4), in_=src[:, :, lo:hi].rearrange("p t (c i) -> p c t i", i=4))
+        def weave(copy, dst, src):
+            copy(out=dst.rearrange("p (c i) t -> p c t i", i=4), in_=src.rearrange("p t (c i) -> p c t i", i=4))
 
 
-        for h in range(2):
+        def drive_product(t, lo, hi, bank):
+            m = slice(t * P, (t + 1) * P)
+            u_ps = psum.tile([P, T], F32, name="u_ps%d" % bank, tag="bank%d" % bank)
+            nc.tensor.matmul_mx(out=u_ps[:, 0 : hi - lo], lhsT=wb_dealt[:, m].bitcast(FP8X4), lhsT_scale=sb_dealt[:, m],
+                                rhs=x_codes[:, lo:hi].bitcast(FP8X4), rhs_scale=x_scales[:, lo:hi], start=True, stop=True)
+            nc.scalar.copy(out=u_sb[t][:, lo:hi], in_=u_ps[:, 0 : hi - lo])
+
+        def quantise_half(h):
             cols = slice(h * HALF, (h + 1) * HALF)
-            weave(nc.vector.tensor_copy, x_bf[h], x_raw[h], 0, HALF)
             nc.vector.quantize_mx(out=x_codes[:, cols].bitcast(FP8X4), scales=x_scales[:, cols], in_=x_bf[h][:].rearrange("p c t -> p (c t)"))
-            for t in range(PACK):
-                m = slice(t * P, (t + 1) * P)
-                u_ps = psum.tile([P, T], F32, name="u_ps%d_%d" % (h, t), tag="bank%d" % (PACK * h + t))
-                nc.tensor.matmul_mx(out=u_ps[:, 0:HALF], lhsT=wb_dealt[:, m].bitcast(FP8X4), lhsT_scale=sb_dealt[:, m],
-                                    rhs=x_codes[:, cols].bitcast(FP8X4), rhs_scale=x_scales[:, cols], start=True, stop=True)
-                nc.scalar.copy(out=u_sb[t][:, cols], in_=u_ps[:, 0:HALF])
-        deal(wa_dealt[:].bitcast(U16), wa_raw[:].bitcast(U16))
-        deal(sa_dealt[:], sa_raw[:], nc.gpsimd)
-        z_ps = [psum.tile([P, T], F32, name="z_ps%d" % t, tag="bank%d" % t) for t in range(PACK)]
+            drive_product(0, h * HALF, (h + 1) * HALF, h)
+
+        weave(nc.scalar.copy, x_bf[0][:, X_SPLIT:HALF, :], x_raw[0][:, :, X_SPLIT:HALF])
+        weave(nc.vector.tensor_copy, x_bf[0][:, 0:X_SPLIT, :], x_raw[0][:, :, 0:X_SPLIT])
+        quantise_half(0)
+        weave(nc.vector.tensor_copy, x_bf[1][:, 0 : HALF // 2, :], x_raw[1][:])
+        weave(nc.vector.tensor_copy, x_bf[1][:, HALF // 2 : HALF, :], x_raw[2][:])
+        quantise_half(1)
+        for t in range(1, PACK):
+            drive_product(t, 0, T, 1 + t)
+        deal(wa_dealt[:].bitcast(U16), wa_raw[:].bitcast(U16), 8)
+        deal(sa_dealt[:], sa_raw[:], 16, nc.gpsimd)
+        z_ps = [psum.tile([P, T], F32, name="z_ps%d" % t, tag="bank%d" % ((5 + t) % 8)) for t in range(PACK)]
         for t in range(PACK):
             nc.tensor.matmul_mx(out=z_ps[t][:], lhsT=wa_dealt[:, 2 * t * P : 2 * (t + 1) * P].bitcast(FP4X4), lhsT_scale=sa_dealt[:, t * P : (t + 1) * P],
                                 rhs=x_codes[:].bitcast(FP8X4), rhs_scale=x_scales[:], start=True, stop=True)
@@ -149,7 +160,7 @@ def tile_list_divided_by_neighbour_pl_kernel(tc, xt, wa_words, wa_scales, wb_wor
                     s = t - 1
                     nc.vector.scalar_tensor_tensor(out=y[:, s, :], in0=own[s][:, lo:hi], scalar=sh_sb[:, s : s + 1], in1=quot[s], op0=ALU.mult, op1=ALU.add)
             nc.sync.dma_start(out=y_rows[:, :, lo:hi], in_=y[:])
-            weave(nc.scalar.copy if c < len(CHUNKS) - 1 else nc.vector.tensor_copy, y_bf, y, 0, w)
+            weave(nc.scalar.copy if c < len(CHUNKS) - 1 else nc.vector.tensor_copy, y_bf[:], y[:])
             nc.vector.quantize_mx(out=y_codes[:, lo:hi].bitcast(FP8X4), scales=y_scales[:, lo:hi], in_=y_bf[:].rearrange("p c t -> p (c t)"))
             nc.sync.dma_start(out=words_out[:, lo:hi], in_=y_codes[:, lo:hi])
         for q in range(4):

@@ -17,12 +17,16 @@ ALU = mybir.AluOpType
 
 P = 128
 PACK = 4
+QUADRANTS = 4
+BANKS = 8
+LIST_ROWS = 16
+LINE_BYTES = 16
 HALF = T // 2
+QUARTER = T // 4
 U_WINDOW = 704
-CHUNKS = ((0, 256), (256, 384), (384, 512))
-X_CHUNKS = ((0, 256), (256, 384), (384, 512))
-X_SPLIT = 160
-ROOT = 1.0625
+CHUNKS = ((0, HALF), (HALF, HALF + QUARTER), (HALF + QUARTER, J))
+QUOTIENT_TILES = 3
+CENTRE = (17.0 / 16.0) ** 2
 
 
 def tile_list_divided_by_neighbour_pl_kernel(tc, xt, wa_words, wa_scales, wb_words, wb_scales, sh, offs, offs2, out_0, out_1, out_2):
@@ -34,135 +38,161 @@ def tile_list_divided_by_neighbour_pl_kernel(tc, xt, wa_words, wa_scales, wb_wor
         def tile(shape, dtype, name, tag=None):
             return keep.tile(shape, dtype, name=name, tag=tag or name, align_bytes=64)
 
-        offs_sb = keep.tile([P, J // 16], U16, name="offs_sb")
-        offs2_sb = keep.tile([P, J // 16], U16, name="offs2_sb")
+        def bank(b, name):
+            return psum.tile([P, T], F32, name=name, tag="bank%d" % b)
 
-        sb_raw = tile([P, N], U8, "sb_raw")
-        sa_raw = tile([P, N], U8, "sa_raw")
-        centre = tile([P, 1], F32, "centre")
-        nc.vector.memset(centre[:], ROOT * ROOT)
+        def scale_rows(plane, q):
+            return plane[:].bitcast(I32)[32 * q : 32 * q + 4, :]
 
-        x_rows = xt.rearrange("(p i) w -> p i w", i=PACK)
-        x_raw = [tile([P, PACK, hi - lo], F32, "x_raw%d" % h) for h, (lo, hi) in enumerate(X_CHUNKS)]
-        wb_raw = tile([P, N], I32, "wb_raw")
-        wa_raw = tile([P, 2 * N], U8, "wa_raw")
-        sh_sb = tile([P, PACK], F32, "sh_sb")
+        def hbm_scale_rows(scales, q):
+            return scales[0].bitcast(I32)[4 * q : 4 * q + 4, :]
 
-        def load_scales(queue, plane, rows):
-            for q in range(4):
-                queue.dma_start(out=plane[:].bitcast(I32)[32 * q : 32 * q + 4, :], in_=rows[0].bitcast(I32)[4 * q : 4 * q + 4, :])
+        def hbm_words(words):
+            return words[0].rearrange("p c r -> p (c r)").bitcast(I32)
 
-        nc.gpsimd.memset(sb_raw[:].bitcast(I32), 0)
-        nc.gpsimd.memset(sa_raw[:].bitcast(I32), 0)
-        nc.sync.dma_start(out=wb_raw[:], in_=wb_words[0].rearrange("p n r -> p (n r)").bitcast(I32))
-        nc.sync.dma_start(out=x_raw[0][:], in_=x_rows[:, :, X_CHUNKS[0][0] : X_CHUNKS[0][1]])
-        load_scales(nc.sync, sb_raw, wb_scales)
-        for h in range(1, len(X_CHUNKS)):
-            nc.sync.dma_start(out=x_raw[h][:], in_=x_rows[:, :, X_CHUNKS[h][0] : X_CHUNKS[h][1]])
-        nc.sync.dma_start(offs2_sb[:], offs2)
-        nc.sync.dma_start(out=wa_raw[:].bitcast(I32), in_=wa_words[0].bitcast(I32))
-        load_scales(nc.sync, sa_raw, wa_scales)
-        nc.sync.dma_start(offs_sb[:], offs)
-        nc.gpsimd.dma_start(out=sh_sb[:], in_=sh.rearrange("(p t) o -> p (t o)", t=PACK))
-
-        warm_in = tile([P, 1], F32, "warm_in")
-        warm_out = tile([P, 1], F32, "warm_out")
-        nc.gpsimd.memset(warm_in[:], 1.0)
-        nc.scalar.activation(out=warm_out[:], in_=warm_in[:], func=ACT.Abs_reciprocal_sqrt)
-
-        u_sb = [tile([P, U_WINDOW], F32, "u_sb%d" % t) for t in range(PACK)]
-        z_sb = [tile([P, T], F32, "z_sb%d" % t) for t in range(PACK)]
-        for t in range(PACK):
-            nc.gpsimd.memset(u_sb[t][:, T:U_WINDOW], 0.0)
-
-        wb_dealt = tile([P, N], I32, "wb_dealt")
-        sb_dealt = tile([P, N], U8, "sb_dealt")
-        wa_dealt = tile([P, 2 * N], U8, "wa_dealt")
-        sa_dealt = tile([P, N], U8, "sa_dealt")
-
-        def deal(dst, src, line, engine=nc.vector):
-            engine.tensor_copy(out=dst.rearrange("p (t a i) -> p a t i", t=PACK, i=line), in_=src.rearrange("p (a i t) -> p a t i", t=PACK, i=line))
-
-        deal(wb_dealt[:], wb_raw[:], 4)
-        deal(sb_dealt[:], sb_raw[:], 16)
-
-        x_bf = [tile([P, HALF, PACK], BF16, "x_bf%d" % h) for h in range(2)]
-        x_codes = tile([P, T], I32, "x_codes")
-        x_scales = tile([P, T], U8, "x_scales")
+        def deal(dst, src, element_bytes, first=0, last=PACK):
+            run = LINE_BYTES // element_bytes
+            nc.vector.tensor_copy(
+                out=dst.rearrange("p (t a i) -> p a t i", t=PACK, i=run)[:, :, first:last, :],
+                in_=src.rearrange("p (a i t) -> p a t i", t=PACK, i=run)[:, :, first:last, :],
+            )
 
         def weave(copy, dst, src):
             copy(out=dst.rearrange("p (c i) t -> p c t i", i=4), in_=src.rearrange("p t (c i) -> p c t i", i=4))
 
+        def quantise(codes, scales, woven):
+            nc.vector.quantize_mx(out=codes.bitcast(FP8X4), scales=scales, in_=woven.rearrange("p c t -> p (c t)"))
 
-        def drive_product(t, lo, hi, bank):
-            m = slice(t * P, (t + 1) * P)
-            u_ps = psum.tile([P, T], F32, name="u_ps%d" % bank, tag="bank%d" % bank)
-            nc.tensor.matmul_mx(out=u_ps[:, 0 : hi - lo], lhsT=wb_dealt[:, m].bitcast(FP8X4), lhsT_scale=sb_dealt[:, m],
-                                rhs=x_codes[:, lo:hi].bitcast(FP8X4), rhs_scale=x_scales[:, lo:hi], start=True, stop=True)
+        offs_sb = keep.tile([P, J // LIST_ROWS], U16, name="offs_sb")
+        offs2_sb = keep.tile([P, J // LIST_ROWS], U16, name="offs2_sb")
+        wb_scales_raw = tile([P, N], U8, "wb_scales_raw")
+        wa_scales_raw = tile([P, N], U8, "wa_scales_raw")
+        centre = tile([P, 1], F32, "centre")
+        nc.vector.memset(centre[:], CENTRE)
+        x_raw = tile([P, PACK, T], F32, "x_raw")
+        wb_raw = tile([P, N], I32, "wb_raw")
+        wa_raw = tile([P, 2 * N], U8, "wa_raw")
+        sh_sb = tile([P, PACK], F32, "sh_sb")
+
+        nc.gpsimd.memset(wb_scales_raw[:].bitcast(I32), 0)
+        nc.gpsimd.memset(wa_scales_raw[:].bitcast(I32), 0)
+        nc.sync.dma_start(out=x_raw[:], in_=xt.rearrange("(p i) w -> p i w", i=PACK))
+        nc.sync.dma_start(out=wb_raw[:], in_=hbm_words(wb_words))
+        for q in range(QUADRANTS):
+            nc.sync.dma_start(out=scale_rows(wb_scales_raw, q), in_=hbm_scale_rows(wb_scales, q))
+        nc.sync.dma_start(out=wa_raw[:].bitcast(I32), in_=wa_words[0].bitcast(I32))
+        nc.sync.dma_start(offs2_sb[:], offs2)
+        for q in range(QUADRANTS):
+            nc.sync.dma_start(out=scale_rows(wa_scales_raw, q), in_=hbm_scale_rows(wa_scales, q))
+        nc.sync.dma_start(offs_sb[:], offs)
+        nc.sync.dma_start(out=sh_sb[:], in_=sh.rearrange("(p t) o -> p (t o)", t=PACK))
+
+        inv_root_centre = tile([P, 1], F32, "inv_root_centre")
+        root_centre = tile([P, 1], F32, "root_centre")
+        nc.scalar.activation(out=inv_root_centre[:], in_=centre[:], func=ACT.Abs_reciprocal_sqrt)
+        nc.vector.reciprocal(out=root_centre[:], in_=inv_root_centre[:])
+
+        u_sb = [tile([P, U_WINDOW], F32, "u_sb%d" % t) for t in range(PACK)]
+        z_sb = [tile([P, T], F32, "z_sb%d" % t) for t in range(PACK)]
+        for t in range(PACK):
+            nc.vector.memset(u_sb[t][:, T:U_WINDOW], 0.0)
+
+        wb_dealt = tile([P, N], I32, "wb_dealt", tag="x_raw")
+        wb_scales_dealt = tile([P, N], U8, "wb_scales_dealt")
+        wa_dealt = tile([P, 2 * N], U8, "wa_dealt", tag="wb_raw")
+        wa_scales_dealt = tile([P, N], U8, "wa_scales_dealt", tag="wa_raw")
+        x_woven = [tile([P, HALF, PACK], BF16, "x_woven%d" % h) for h in range(2)]
+        x_codes = tile([P, T], I32, "x_codes")
+        x_scales = tile([P, T], U8, "x_scales")
+
+        def drive_product(t, lo, hi, b):
+            features = slice(t * P, (t + 1) * P)
+            u_ps = bank(b, "u_ps%d" % b)
+            nc.tensor.matmul_mx(
+                out=u_ps[:, 0 : hi - lo],
+                lhsT=wb_dealt[:, features].bitcast(FP8X4), lhsT_scale=wb_scales_dealt[:, features],
+                rhs=x_codes[:, lo:hi].bitcast(FP8X4), rhs_scale=x_scales[:, lo:hi],
+                start=True, stop=True,
+            )
             nc.scalar.copy(out=u_sb[t][:, lo:hi], in_=u_ps[:, 0 : hi - lo])
 
-        def quantise_half(h):
-            cols = slice(h * HALF, (h + 1) * HALF)
-            nc.vector.quantize_mx(out=x_codes[:, cols].bitcast(FP8X4), scales=x_scales[:, cols], in_=x_bf[h][:].rearrange("p c t -> p (c t)"))
-            drive_product(0, h * HALF, (h + 1) * HALF, h)
+        weave(nc.scalar.copy, x_woven[1][:, QUARTER:HALF, :], x_raw[:, :, T - QUARTER : T])
+        weave(nc.vector.tensor_copy, x_woven[0][:], x_raw[:, :, 0:HALF])
+        weave(nc.vector.tensor_copy, x_woven[1][:, 0:QUARTER, :], x_raw[:, :, HALF : T - QUARTER])
 
-        weave(nc.scalar.copy, x_bf[0][:, X_SPLIT:HALF, :], x_raw[0][:, :, X_SPLIT:HALF])
-        weave(nc.vector.tensor_copy, x_bf[0][:, 0:X_SPLIT, :], x_raw[0][:, :, 0:X_SPLIT])
-        quantise_half(0)
-        weave(nc.vector.tensor_copy, x_bf[1][:, 0 : HALF // 2, :], x_raw[1][:])
-        weave(nc.vector.tensor_copy, x_bf[1][:, HALF // 2 : HALF, :], x_raw[2][:])
-        quantise_half(1)
+        quantise(x_codes[:, 0:HALF], x_scales[:, 0:HALF], x_woven[0][:])
+        deal(wb_dealt[:], wb_raw[:], 4, 0, 1)
+        deal(wb_scales_dealt[:], wb_scales_raw[:], 1, 0, 1)
+        drive_product(0, 0, HALF, 0)
+        quantise(x_codes[:, HALF:T], x_scales[:, HALF:T], x_woven[1][:])
+        drive_product(0, HALF, T, 1)
+        deal(wb_dealt[:], wb_raw[:], 4, 1, PACK)
+        deal(wb_scales_dealt[:], wb_scales_raw[:], 1, 1, PACK)
         for t in range(1, PACK):
             drive_product(t, 0, T, 1 + t)
-        deal(wa_dealt[:].bitcast(U16), wa_raw[:].bitcast(U16), 8)
-        deal(sa_dealt[:], sa_raw[:], 16, nc.gpsimd)
-        z_ps = [psum.tile([P, T], F32, name="z_ps%d" % t, tag="bank%d" % ((5 + t) % 8)) for t in range(PACK)]
-        for t in range(PACK):
-            nc.tensor.matmul_mx(out=z_ps[t][:], lhsT=wa_dealt[:, 2 * t * P : 2 * (t + 1) * P].bitcast(FP4X4), lhsT_scale=sa_dealt[:, t * P : (t + 1) * P],
-                                rhs=x_codes[:].bitcast(FP8X4), rhs_scale=x_scales[:], start=True, stop=True)
 
-        drive = [tile([P, J], F32, "drive%d" % t, tag="wa_raw" if t == 0 else None) for t in range(PACK)]
-        own = [tile([P, J], F32, "own%d" % t) for t in range(PACK)]
-        pos = [tile([P, J], F32, "pos%d" % t) for t in range(PACK)]
-        root = [tile([P, J], F32, "root%d" % t) for t in range(PACK)]
+        deal(wa_dealt[:].bitcast(U16), wa_raw[:].bitcast(U16), 2)
+        deal(wa_scales_dealt[:], wa_scales_raw[:], 1)
+        z_ps = [bank((1 + PACK + t) % BANKS, "z_ps%d" % t) for t in range(PACK)]
+        for t in range(PACK):
+            nc.tensor.matmul_mx(
+                out=z_ps[t][:],
+                lhsT=wa_dealt[:, 2 * t * P : 2 * (t + 1) * P].bitcast(FP4X4), lhsT_scale=wa_scales_dealt[:, t * P : (t + 1) * P],
+                rhs=x_codes[:].bitcast(FP8X4), rhs_scale=x_scales[:],
+                start=True, stop=True,
+            )
+
+        neighbour = [tile([P, J], F32, "neighbour%d" % t) for t in range(PACK)]
+        own = [tile([P, J], F32, "own%d" % t, tag="wa_scales_raw" if t == 0 else None) for t in range(PACK)]
+        positive = [tile([P, J], F32, "positive%d" % t) for t in range(PACK)]
+        inv_root = [tile([P, J], F32, "inv_root%d" % t) for t in range(PACK)]
         gain = [tile([P, J], F32, "gain%d" % t) for t in range(PACK)]
         for t in range(PACK):
-            nc.vector.tensor_copy(out=drive[t][:], in_=u_sb[t][:].indirect(offs2_sb[:]))
-        for t in range(PACK):
-            nc.scalar.copy(out=z_sb[t][:], in_=z_ps[t][:])
+            nc.vector.tensor_copy(out=neighbour[t][:], in_=u_sb[t][:].indirect(offs2_sb[:]))
         for t in range(PACK):
             nc.vector.tensor_copy(out=own[t][:], in_=u_sb[t][:].indirect(offs_sb[:]))
+
         for step in range(PACK + 2):
             if step < PACK:
-                nc.scalar.activation(out=pos[step][:], in_=drive[step][:], func=ACT.Relu)
+                nc.scalar.activation(out=positive[step][:], in_=neighbour[step][:], func=ACT.Relu)
             if 1 <= step <= PACK:
-                nc.scalar.activation(out=root[step - 1][:], in_=pos[step - 1][:], func=ACT.Abs_reciprocal_sqrt, scale=ROOT * ROOT, bias=centre[:])
+                nc.scalar.activation(out=inv_root[step - 1][:], in_=positive[step - 1][:], func=ACT.Abs_reciprocal_sqrt, scale=CENTRE, bias=centre[:])
             if step >= 2:
-                nc.scalar.activation(out=gain[step - 2][:], in_=root[step - 2][:], func=ACT.Square, scale=ROOT)
+                nc.scalar.activation(out=gain[step - 2][:], in_=inv_root[step - 2][:], func=ACT.Square, scale=root_centre[:])
+        for t in range(PACK):
+            nc.scalar.copy(out=z_sb[t][:], in_=z_ps[t][:])
 
         y_rows = out_0.rearrange("(p t) j -> p t j", t=PACK)
         y_codes = tile([P, J], I32, "y_codes")
         y_scales = tile([P, J], U8, "y_scales")
-        words_out = out_1[0].rearrange("p c r -> p (c r)").bitcast(I32)
-        ring = [tile([P, HALF], F32, "quot%d" % r) for r in range(3)]
+        ring = [tile([P, HALF], F32, "quotient%d" % r) for r in range(QUOTIENT_TILES)]
         for c, (lo, hi) in enumerate(CHUNKS):
-            w = hi - lo
-            y = tile([P, PACK, w], F32, "y%d" % c)
-            y_bf = tile([P, w, PACK], BF16, "y_bf%d" % c)
-            quot = [ring[(PACK * c + t) % 3][:, 0:w] for t in range(PACK)]
-            if c == 2:
-                quot[0] = tile([P, w], F32, "quot_a", tag="y_bf0")[:]
-                quot[3] = tile([P, w], F32, "quot_b", tag="y_bf1")[:]
+            width = hi - lo
+            last_chunk = hi == J
+            y = tile([P, PACK, width], F32, "y%d" % c)
+            y_woven = tile([P, width, PACK], BF16, "y_woven%d" % c, tag="y_woven%d" % (c - 1) if last_chunk else None)
+            quotient = [ring[(PACK * c + t) % QUOTIENT_TILES][:, 0:width] for t in range(PACK)]
+            if last_chunk:
+                quotient[0] = tile([P, width], F32, "quotient_last", tag="y_woven0")[:]
             for t in range(PACK + 1):
                 if t < PACK:
-                    nc.vector.tensor_tensor(out=quot[t], in0=z_sb[t][:].indirect(offs_sb[:, lo // 16 : hi // 16]), in1=gain[t][:, lo:hi], op=ALU.mult)
+                    entries = offs_sb[:, lo // LIST_ROWS : hi // LIST_ROWS]
+                    nc.vector.tensor_tensor(out=quotient[t], in0=z_sb[t][:].indirect(entries), in1=gain[t][:, lo:hi], op=ALU.mult)
                 if t > 0:
-                    s = t - 1
-                    nc.vector.scalar_tensor_tensor(out=y[:, s, :], in0=own[s][:, lo:hi], scalar=sh_sb[:, s : s + 1], in1=quot[s], op0=ALU.mult, op1=ALU.add)
+                    nc.vector.scalar_tensor_tensor(
+                        out=y[:, t - 1, :], in0=own[t - 1][:, lo:hi], scalar=sh_sb[:, t - 1 : t], in1=quotient[t - 1],
+                        op0=ALU.mult, op1=ALU.add,
+                    )
             nc.sync.dma_start(out=y_rows[:, :, lo:hi], in_=y[:])
-            weave(nc.scalar.copy if c < len(CHUNKS) - 1 else nc.vector.tensor_copy, y_bf[:], y[:])
-            nc.vector.quantize_mx(out=y_codes[:, lo:hi].bitcast(FP8X4), scales=y_scales[:, lo:hi], in_=y_bf[:].rearrange("p c t -> p (c t)"))
-            nc.sync.dma_start(out=words_out[:, lo:hi], in_=y_codes[:, lo:hi])
-        for q in range(4):
+
+            parts = ((0, width // 2), (width // 2, width)) if last_chunk else ((0, width),)
+            for a, b in parts:
+                weave(nc.vector.tensor_copy if last_chunk else nc.scalar.copy, y_woven[:, a:b, :], y[:, :, a:b])
+            for a, b in parts:
+                quantise(y_codes[:, lo + a : lo + b], y_scales[:, lo + a : lo + b], y_woven[:, a:b, :])
+            if hi % HALF == 0:
+                nc.sync.dma_start(out=hbm_words(out_1)[:, hi - HALF : hi], in_=y_codes[:, hi - HALF : hi])
+
+        for q in range(QUADRANTS):
             queue = nc.scalar if q % 2 == 0 else nc.sync
-            queue.dma_start(out=out_2[0].bitcast(I32)[4 * q : 4 * q + 4, :], in_=y_scales[:].bitcast(I32)[32 * q : 32 * q + 4, :])
+            queue.dma_start(out=hbm_scale_rows(out_2, q), in_=scale_rows(y_scales, q))

from contextlib import ExitStack

import concourse.mybir as mybir

K, T, J, N = 512, 512, 512, 512
FLOPS = 2 * 2 * K * N * T

F32 = mybir.dt.float32
BF16 = mybir.dt.bfloat16
I32 = mybir.dt.int32
U16 = mybir.dt.uint16
U8 = mybir.dt.uint8
FP8X4 = mybir.dt.float8_e4m3fn_x4
FP4X4 = mybir.dt.float4_e2m1fn_x4
ACT = mybir.ActivationFunctionType
ALU = mybir.AluOpType

P = 128
PACK = 4
QUADRANTS = 4
BANKS = 8
LIST_ROWS = 16
LINE_BYTES = 16
HALF = T // 2
QUARTER = T // 4
U_WINDOW = 704
CHUNKS = ((0, HALF), (HALF, HALF + QUARTER), (HALF + QUARTER, J))
QUOTIENT_TILES = 3
CENTRE = (17.0 / 16.0) ** 2


def tile_list_divided_by_neighbour_pl_kernel(tc, xt, wa_words, wa_scales, wb_words, wb_scales, sh, offs, offs2, out_0, out_1, out_2):
    nc = tc.nc
    with ExitStack() as ctx:
        keep = ctx.enter_context(tc.tile_pool(name="keep", bufs=1))
        psum = ctx.enter_context(tc.psum_pool(name="psum", bufs=1))

        def tile(shape, dtype, name, tag=None):
            return keep.tile(shape, dtype, name=name, tag=tag or name, align_bytes=64)

        def bank(b, name):
            return psum.tile([P, T], F32, name=name, tag="bank%d" % b)

        def scale_rows(plane, q):
            return plane[:].bitcast(I32)[32 * q : 32 * q + 4, :]

        def hbm_scale_rows(scales, q):
            return scales[0].bitcast(I32)[4 * q : 4 * q + 4, :]

        def hbm_words(words):
            return words[0].rearrange("p c r -> p (c r)").bitcast(I32)

        def deal(dst, src, element_bytes, first=0, last=PACK):
            run = LINE_BYTES // element_bytes
            nc.vector.tensor_copy(
                out=dst.rearrange("p (t a i) -> p a t i", t=PACK, i=run)[:, :, first:last, :],
                in_=src.rearrange("p (a i t) -> p a t i", t=PACK, i=run)[:, :, first:last, :],
            )

        def weave(copy, dst, src):
            copy(out=dst.rearrange("p (c i) t -> p c t i", i=4), in_=src.rearrange("p t (c i) -> p c t i", i=4))

        def quantise(codes, scales, woven):
            nc.vector.quantize_mx(out=codes.bitcast(FP8X4), scales=scales, in_=woven.rearrange("p c t -> p (c t)"))

        offs_sb = keep.tile([P, J // LIST_ROWS], U16, name="offs_sb")
        offs2_sb = keep.tile([P, J // LIST_ROWS], U16, name="offs2_sb")
        wb_scales_raw = tile([P, N], U8, "wb_scales_raw")
        wa_scales_raw = tile([P, N], U8, "wa_scales_raw")
        centre = tile([P, 1], F32, "centre")
        nc.vector.memset(centre[:], CENTRE)
        x_raw = tile([P, PACK, T], F32, "x_raw")
        wb_raw = tile([P, N], I32, "wb_raw")
        wa_raw = tile([P, 2 * N], U8, "wa_raw")
        sh_sb = tile([P, PACK], F32, "sh_sb")

        nc.gpsimd.memset(wb_scales_raw[:].bitcast(I32), 0)
        nc.gpsimd.memset(wa_scales_raw[:].bitcast(I32), 0)
        nc.sync.dma_start(out=x_raw[:], in_=xt.rearrange("(p i) w -> p i w", i=PACK))
        nc.sync.dma_start(out=wb_raw[:], in_=hbm_words(wb_words))
        for q in range(QUADRANTS):
            nc.sync.dma_start(out=scale_rows(wb_scales_raw, q), in_=hbm_scale_rows(wb_scales, q))
        nc.sync.dma_start(out=wa_raw[:].bitcast(I32), in_=wa_words[0].bitcast(I32))
        nc.sync.dma_start(offs2_sb[:], offs2)
        for q in range(QUADRANTS):
            nc.sync.dma_start(out=scale_rows(wa_scales_raw, q), in_=hbm_scale_rows(wa_scales, q))
        nc.sync.dma_start(offs_sb[:], offs)
        nc.sync.dma_start(out=sh_sb[:], in_=sh.rearrange("(p t) o -> p (t o)", t=PACK))

        inv_root_centre = tile([P, 1], F32, "inv_root_centre")
        root_centre = tile([P, 1], F32, "root_centre")
        nc.scalar.activation(out=inv_root_centre[:], in_=centre[:], func=ACT.Abs_reciprocal_sqrt)
        nc.vector.reciprocal(out=root_centre[:], in_=inv_root_centre[:])

        u_sb = [tile([P, U_WINDOW], F32, "u_sb%d" % t) for t in range(PACK)]
        z_sb = [tile([P, T], F32, "z_sb%d" % t) for t in range(PACK)]
        for t in range(PACK):
            nc.vector.memset(u_sb[t][:, T:U_WINDOW], 0.0)

        wb_dealt = tile([P, N], I32, "wb_dealt", tag="x_raw")
        wb_scales_dealt = tile([P, N], U8, "wb_scales_dealt")
        wa_dealt = tile([P, 2 * N], U8, "wa_dealt", tag="wb_raw")
        wa_scales_dealt = tile([P, N], U8, "wa_scales_dealt", tag="wa_raw")
        x_woven = [tile([P, HALF, PACK], BF16, "x_woven%d" % h) for h in range(2)]
        x_codes = tile([P, T], I32, "x_codes")
        x_scales = tile([P, T], U8, "x_scales")

        def drive_product(t, lo, hi, b):
            features = slice(t * P, (t + 1) * P)
            u_ps = bank(b, "u_ps%d" % b)
            nc.tensor.matmul_mx(
                out=u_ps[:, 0 : hi - lo],
                lhsT=wb_dealt[:, features].bitcast(FP8X4), lhsT_scale=wb_scales_dealt[:, features],
                rhs=x_codes[:, lo:hi].bitcast(FP8X4), rhs_scale=x_scales[:, lo:hi],
                start=True, stop=True,
            )
            nc.scalar.copy(out=u_sb[t][:, lo:hi], in_=u_ps[:, 0 : hi - lo])

        weave(nc.scalar.copy, x_woven[1][:, QUARTER:HALF, :], x_raw[:, :, T - QUARTER : T])
        weave(nc.vector.tensor_copy, x_woven[0][:], x_raw[:, :, 0:HALF])
        weave(nc.vector.tensor_copy, x_woven[1][:, 0:QUARTER, :], x_raw[:, :, HALF : T - QUARTER])

        quantise(x_codes[:, 0:HALF], x_scales[:, 0:HALF], x_woven[0][:])
        deal(wb_dealt[:], wb_raw[:], 4, 0, 1)
        deal(wb_scales_dealt[:], wb_scales_raw[:], 1, 0, 1)
        drive_product(0, 0, HALF, 0)
        quantise(x_codes[:, HALF:T], x_scales[:, HALF:T], x_woven[1][:])
        drive_product(0, HALF, T, 1)
        deal(wb_dealt[:], wb_raw[:], 4, 1, PACK)
        deal(wb_scales_dealt[:], wb_scales_raw[:], 1, 1, PACK)
        for t in range(1, PACK):
            drive_product(t, 0, T, 1 + t)

        deal(wa_dealt[:].bitcast(U16), wa_raw[:].bitcast(U16), 2)
        deal(wa_scales_dealt[:], wa_scales_raw[:], 1)
        z_ps = [bank((1 + PACK + t) % BANKS, "z_ps%d" % t) for t in range(PACK)]
        for t in range(PACK):
            nc.tensor.matmul_mx(
                out=z_ps[t][:],
                lhsT=wa_dealt[:, 2 * t * P : 2 * (t + 1) * P].bitcast(FP4X4), lhsT_scale=wa_scales_dealt[:, t * P : (t + 1) * P],
                rhs=x_codes[:].bitcast(FP8X4), rhs_scale=x_scales[:],
                start=True, stop=True,
            )

        neighbour = [tile([P, J], F32, "neighbour%d" % t) for t in range(PACK)]
        own = [tile([P, J], F32, "own%d" % t, tag="wa_scales_raw" if t == 0 else None) for t in range(PACK)]
        positive = [tile([P, J], F32, "positive%d" % t) for t in range(PACK)]
        inv_root = [tile([P, J], F32, "inv_root%d" % t) for t in range(PACK)]
        gain = [tile([P, J], F32, "gain%d" % t) for t in range(PACK)]
        for t in range(PACK):
            nc.vector.tensor_copy(out=neighbour[t][:], in_=u_sb[t][:].indirect(offs2_sb[:]))
        for t in range(PACK):
            nc.vector.tensor_copy(out=own[t][:], in_=u_sb[t][:].indirect(offs_sb[:]))

        for step in range(PACK + 2):
            if step < PACK:
                nc.scalar.activation(out=positive[step][:], in_=neighbour[step][:], func=ACT.Relu)
            if 1 <= step <= PACK:
                nc.scalar.activation(out=inv_root[step - 1][:], in_=positive[step - 1][:], func=ACT.Abs_reciprocal_sqrt, scale=CENTRE, bias=centre[:])
            if step >= 2:
                nc.scalar.activation(out=gain[step - 2][:], in_=inv_root[step - 2][:], func=ACT.Square, scale=root_centre[:])
        for t in range(PACK):
            nc.scalar.copy(out=z_sb[t][:], in_=z_ps[t][:])

        y_rows = out_0.rearrange("(p t) j -> p t j", t=PACK)
        y_codes = tile([P, J], I32, "y_codes")
        y_scales = tile([P, J], U8, "y_scales")
        ring = [tile([P, HALF], F32, "quotient%d" % r) for r in range(QUOTIENT_TILES)]
        for c, (lo, hi) in enumerate(CHUNKS):
            width = hi - lo
            last_chunk = hi == J
            y = tile([P, PACK, width], F32, "y%d" % c)
            y_woven = tile([P, width, PACK], BF16, "y_woven%d" % c, tag="y_woven%d" % (c - 1) if last_chunk else None)
            quotient = [ring[(PACK * c + t) % QUOTIENT_TILES][:, 0:width] for t in range(PACK)]
            if last_chunk:
                quotient[0] = tile([P, width], F32, "quotient_last", tag="y_woven0")[:]
            for t in range(PACK + 1):
                if t < PACK:
                    entries = offs_sb[:, lo // LIST_ROWS : hi // LIST_ROWS]
                    nc.vector.tensor_tensor(out=quotient[t], in0=z_sb[t][:].indirect(entries), in1=gain[t][:, lo:hi], op=ALU.mult)
                if t > 0:
                    nc.vector.scalar_tensor_tensor(
                        out=y[:, t - 1, :], in0=own[t - 1][:, lo:hi], scalar=sh_sb[:, t - 1 : t], in1=quotient[t - 1],
                        op0=ALU.mult, op1=ALU.add,
                    )
            nc.sync.dma_start(out=y_rows[:, :, lo:hi], in_=y[:])

            parts = ((0, width // 2), (width // 2, width)) if last_chunk else ((0, width),)
            for a, b in parts:
                weave(nc.vector.tensor_copy if last_chunk else nc.scalar.copy, y_woven[:, a:b, :], y[:, :, a:b])
            for a, b in parts:
                quantise(y_codes[:, lo + a : lo + b], y_scales[:, lo + a : lo + b], y_woven[:, a:b, :])
            if hi % HALF == 0:
                nc.sync.dma_start(out=hbm_words(out_1)[:, hi - HALF : hi], in_=y_codes[:, hi - HALF : hi])

        for q in range(QUADRANTS):
            queue = nc.scalar if q % 2 == 0 else nc.sync
            queue.dma_start(out=hbm_scale_rows(out_2, q), in_=scale_rows(y_scales, q))
